import numpy as np
import ml_dtypes


def mxq(x, axis, fmt="e4m3"):
    dtype, down = {"e4m3": (ml_dtypes.float8_e4m3fn, 7), "e5m2": (ml_dtypes.float8_e5m2, 14)}[fmt]
    v = np.moveaxis(np.asarray(x, np.float32).astype(ml_dtypes.bfloat16).astype(np.float64), axis, -1)
    blocks = v.reshape(v.shape[:-1] + (-1, 32))
    amax = np.abs(blocks).max(-1, keepdims=True)
    byte = np.maximum(np.where(amax > 0, np.frexp(amax)[1] - 1 + 127, 0) - down, 1)
    scale = np.exp2(byte - 127.0)
    codes = (blocks / scale).astype(np.float32).astype(dtype).astype(np.float64)
    return np.moveaxis((codes * scale).reshape(v.shape), -1, axis)


WIDE = False


def mx_kscale(k):
    if not WIDE:
        return np.ones(k)
    levels = np.array([10, -10, 5, -5, 0])
    if k % 512:
        return np.exp2(np.random.permutation(np.resize(levels, k // 32))).repeat(32)
    a = np.empty((k // 512, 16))
    for p in range(k // 512):
        a[p, :8] = np.random.permutation(np.resize(levels, 8))
        for g in range(8):
            far = levels[np.abs(levels - a[p, g]) >= 10]
            a[p, g + 8] = far[np.random.randint(len(far))]
    return np.exp2(a.ravel()).repeat(32)


def f64(x):
    return np.asarray(x).astype(np.float64)


def striped(idx):
    return np.tile(idx.reshape(-1, 16).T, (8, 1)).astype(np.uint16)


def unstriped(offs):
    return offs[:16].T.reshape(-1).astype(np.int64)


E2M1 = np.array([0.0, 0.5, 1.0, 1.5, 2.0, 3.0, 4.0, 6.0, -0.0, -0.5, -1.0, -1.5, -2.0, -3.0, -4.0, -6.0])


def pack_weight(w, fmt):
    k, n = w.shape
    w = f64(np.asarray(w, np.float32).astype(ml_dtypes.bfloat16)).reshape(k // 32, 32, n)
    amax = np.abs(w).max(1)
    if fmt == "e4m3":
        byte = np.frexp(amax)[1] - 1 + 127 - 7
    else:
        mant, ex = np.frexp(amax / 6.0)
        byte = np.where(mant > 0.5, ex, ex - 1) + 127
    byte = np.clip(np.where(amax > 0, byte, 1), 1, 254)
    scaled = (w * np.exp2(127.0 - byte)[:, None, :]).reshape(k, n).astype(np.float32)
    by_word = np.ascontiguousarray(scaled.reshape(k // 512, 128, 4, n).transpose(0, 1, 3, 2))
    if fmt == "e4m3":
        words = by_word.astype(ml_dtypes.float8_e4m3fn).view(np.uint8)
    else:
        c = by_word.astype(ml_dtypes.float4_e2m1fn).view(np.uint8) & 0xF
        words = (c[..., 0::2] | (c[..., 1::2] << 4)).reshape(k // 512, 128, 2 * n)
    return np.ascontiguousarray(words), np.ascontiguousarray(byte.astype(np.uint8).reshape(k // 512, 16, n))


def unpack_weight(words, scales, fmt):
    g, _, n = scales.shape
    words = np.ascontiguousarray(words).reshape(g, 128, n, -1)
    if fmt == "e4m3":
        vals = words.view(ml_dtypes.float8_e4m3fn).astype(np.float64)
    else:
        nib = np.empty((g, 128, n, 4), np.uint8)
        nib[..., 0::2] = words & 0xF
        nib[..., 1::2] = words >> 4
        vals = E2M1[nib]
    vals = vals * np.repeat(np.exp2(scales.astype(np.float64) - 127.0), 8, axis=1)[..., None]
    return vals.transpose(0, 1, 3, 2).reshape(g * 512, n)


def relu(v):
    return np.maximum(v, 0.0)


K, T, E, C, H, N = 512, 1024, 2, 256, 1024, 128


def by_expert(wq, xq):
    return np.concatenate([wq[e].T @ xq[:, e * C:(e + 1) * C] for e in range(E)], axis=1)


def setup_inputs():
    n = np.random.standard_normal
    s = mx_kscale(K)[:, None]
    u = mx_kscale(H)
    w1 = [pack_weight(m, "e2m1") for m in n((E + 1, K, H)) / np.sqrt(K) / s[None]]
    w3 = [pack_weight(m, "e2m1") for m in n((E + 1, K, H)) / np.sqrt(K) / s[None] * u[None, None, :]]
    w2 = [pack_weight(m, "e2m1") for m in n((E + 1, H, N)) / np.sqrt(H) / u[None, :, None]]
    x = pack_weight(n((K, T)) * s, "e4m3")
    return {
        "x_words": x[0],
        "x_scales": x[1],
        "w1_words": np.stack([m[0] for m in w1]),
        "w1_scales": np.stack([m[1] for m in w1]),
        "w3_words": np.stack([m[0] for m in w3]),
        "w3_scales": np.stack([m[1] for m in w3]),
        "w2_words": np.stack([m[0] for m in w2]),
        "w2_scales": np.stack([m[1] for m in w2]),
        "gate": np.tile(np.random.uniform(0.2, 1.0, E * C), (N, 1)).astype(np.float32),
        "offs": striped(np.random.permutation(T)[:E * C]),
    }


def reference(x_words, x_scales, w1_words, w1_scales, w3_words, w3_scales, w2_words, w2_scales, gate, offs):
    idx = unstriped(offs)
    w1 = np.stack([unpack_weight(w1_words[e], w1_scales[e], "e2m1") for e in range(E + 1)])
    w3 = np.stack([unpack_weight(w3_words[e], w3_scales[e], "e2m1") for e in range(E + 1)])
    w2 = np.stack([unpack_weight(w2_words[e], w2_scales[e], "e2m1") for e in range(E + 1)])
    w1q, w3q, w2q = w1, w3, w2
    xs = unpack_weight(x_words, x_scales, "e4m3")
    hs = relu(w1q[E].T @ xs) * (w3q[E].T @ xs)
    ys = w2q[E].T @ mxq(hs, 0, "e4m3")
    xq = unpack_weight(x_words, x_scales, "e4m3")[:, idx]
    h = relu(by_expert(w1q, xq))
    h = h * by_expert(w3q, xq)
    y = by_expert(w2q, mxq(h, 0, "e4m3"))
    out = ys
    out[:, idx] += f64(gate) * y
    return out

@@ -1,0 +1,194 @@
+from contextlib import ExitStack
+
+import concourse.mybir as mybir
+from concourse.masks import make_identity
+
+K, T, E, C, H, N = 512, 1024, 2, 256, 1024, 128
+S = E * C
+
+F32 = mybir.dt.float32
+BF16 = mybir.dt.bfloat16
+I32 = mybir.dt.int32
+U32 = mybir.dt.uint32
+U16 = mybir.dt.uint16
+U8 = mybir.dt.uint8
+FP8X4 = mybir.dt.float8_e4m3fn_x4
+FP4X4 = mybir.dt.float4_e2m1fn_x4
+MULT = mybir.AluOpType.mult
+ADD = mybir.AluOpType.add
+RELU = mybir.ActivationFunctionType.Relu
+
+P = 128
+PASS = 512
+PASSES = H // PASS
+FLOPS = 2 * (S + T) * (2 * K * H + H * N)
+
+
+def tile_moe_shr_glu_relu_kernel(
+    tc, x_words, x_scales, w1_words, w1_scales, w3_words, w3_scales, w2_words, w2_scales, gate, offs, out
+):
+    nc = tc.nc
+    with ExitStack() as ctx:
+        keep = ctx.enter_context(tc.tile_pool(name="keep", bufs=1))
+        ring = ctx.enter_context(tc.tile_pool(name="ring", bufs=3))
+        psum = ctx.enter_context(tc.psum_pool(name="psum", bufs=2))
+
+        def zeroed_plane(name, shape):
+            plane = keep.tile(shape, U8, name=name, align_bytes=64)
+            nc.vector.memset(plane[:].bitcast(I32), 0)
+            return plane
+
+        def load_scale_rows(plane, rows):
+            for r in range(4):
+                nc.sync.dma_start(plane[r:P:32].bitcast(I32), rows[r:16:4].bitcast(I32))
+
+        def load_words(name, src):
+            words = keep.tile([P, 2 * H], U8, name=name, align_bytes=64)
+            nc.sync.dma_start(words[:].bitcast(I32), src.bitcast(I32))
+            return words
+
+        xs = zeroed_plane("xs", [P, T])
+        w1s_first = zeroed_plane("w1s_first", [P, 1, H])
+        w3s_first = zeroed_plane("w3s_first", [P, 1, H])
+        w1s_rest = zeroed_plane("w1s_rest", [P, E, H])
+        w3s_rest = zeroed_plane("w3s_rest", [P, E, H])
+        w2s = zeroed_plane("w2s", [P, (E + 1) * PASSES, N])
+        routed = keep.tile([P, T], F32, name="routed")
+        nc.vector.memset(routed[:], 0.0)
+        ident = keep.tile([P, P], F32, name="ident")
+        make_identity(nc, ident[:])
+
+        xw = keep.tile([P, T], I32, name="xw", align_bytes=64)
+        nc.sync.dma_start(xw[:], x_words[0].rearrange("p t r -> p (t r)").bitcast(I32))
+        offsets = keep.tile([P, S // 16], U16, name="offsets")
+        nc.sync.dma_start(offsets[:], offs)
+        load_scale_rows(xs, x_scales[0])
+        w1w = [load_words("w1w0", w1_words[0, 0])]
+        w3w = [load_words("w3w0", w3_words[0, 0])]
+        w1_rows = w1_scales[:, 0].rearrange("e q i -> q e i")
+        w3_rows = w3_scales[:, 0].rearrange("e q i -> q e i")
+        load_scale_rows(w1s_first, w1_rows[:, 0:1, :])
+        load_scale_rows(w3s_first, w3_rows[:, 0:1, :])
+        load_scale_rows(w1s_rest, w1_rows[:, 1:, :])
+        load_scale_rows(w3s_rest, w3_rows[:, 1:, :])
+        w1w.append(load_words("w1w1", w1_words[1, 0]))
+        w3w.append(load_words("w3w1", w3_words[1, 0]))
+        w2w = keep.tile([P, (E + 1) * PASSES, 2 * N], U8, name="w2w", align_bytes=64)
+        nc.sync.dma_start(w2w[:].bitcast(I32), w2_words.rearrange("e s p n -> p (e s) n").bitcast(I32))
+        load_scale_rows(w2s, w2_scales.rearrange("e s q n -> q (e s) n"))
+        w1w.append(load_words("w1w2", w1_words[2, 0]))
+        w3w.append(load_words("w3w2", w3_words[2, 0]))
+        gates = keep.tile([P, S], F32, name="gates")
+        nc.sync.dma_start(gates[:], gate)
+        w1s = [w1s_first[:, 0, :], w1s_rest[:, 0, :], w1s_rest[:, 1, :]]
+        w3s = [w3s_first[:, 0, :], w3s_rest[:, 0, :], w3s_rest[:, 1, :]]
+
+        tiles = []
+        for first, count in ((0, P), (P, P), (2 * P, 2 * P)):
+            gw = keep.tile([P, count], I32, name=f"gw{first}", align_bytes=64)
+            gs = keep.tile([P, count], U8, name=f"gs{first}", align_bytes=64)
+            piece = offsets[:, first // 16 : (first + count) // 16]
+            nc.vector.tensor_copy(gw[:].bitcast(U32), xw[:].bitcast(U32).indirect(piece))
+            nc.vector.tensor_copy(gs[:], xs[:].indirect(piece))
+            for c in range(0, count, P):
+                tiles.append((gw[:, c : c + P], gs[:, c : c + P], (first + c) // C))
+        n_routed = len(tiles)
+        for c in range(0, T, P):
+            tiles.append((xw[:, c : c + P], xs[:, c : c + P], E))
+
+        def order(ap):
+            return ap.rearrange("t (p u e) -> t u p e", u=2, e=2)
+
+        def plain(ap):
+            return ap.rearrange("t (u p e) -> t u p e", u=2, e=2)
+
+        hidden, turned, quantised, y_bank = {}, {}, {}, {}
+
+        def first_layer(j):
+            words, scales, e = tiles[j]
+            h = ring.tile([P, PASSES, PASS], BF16, name="h", align_bytes=64)
+            for s in range(PASSES):
+                a = psum.tile([P, PASS], F32, name="a", bufs=2)
+                b = psum.tile([P, PASS], F32, name="b", bufs=3)
+                for acc, ww, ws in ((a, w1w[e], w1s[e]), (b, w3w[e], w3s[e])):
+                    nc.tensor.matmul_mx(
+                        acc[:],
+                        lhsT=words.bitcast(FP8X4),
+                        lhsT_scale=scales,
+                        rhs=ww[:, 2 * PASS * s : 2 * PASS * (s + 1)].bitcast(FP4X4),
+                        rhs_scale=ws[:, PASS * s : PASS * (s + 1)],
+                        start=True,
+                        stop=True,
+                    )
+                relu_a = ring.tile([P, PASS], F32, name="relu_a")
+                nc.scalar.activation(plain(relu_a[:]), order(a[:]), RELU)
+                nc.vector.tensor_tensor(plain(h[:, s, :]), order(b[:]), plain(relu_a[:]), MULT)
+            hidden[j] = h
+
+        def turn(j):
+            h = hidden[j]
+            t_ps = psum.tile([P, PASSES * 2, P], F32, name="t_ps", bufs=1)
+            for s in range(PASSES):
+                pairs = h[:, s, :].bitcast(F32)
+                for u in range(2):
+                    nc.tensor.transpose(t_ps[:, 2 * s + u, :], pairs[:, P * u : P * (u + 1)], ident[:])
+            ht = ring.tile([P, PASSES * PASS], BF16, name="ht", align_bytes=64)
+            nc.scalar.copy(
+                ht[:].bitcast(F32).rearrange("p (s t u) -> p s t u", s=PASSES, u=2),
+                t_ps[:].rearrange("p (s u) t -> p s t u", u=2),
+            )
+            turned[j] = ht
+
+        def quantise(j):
+            codes = ring.tile([P, PASSES * P], U32, name="codes", align_bytes=64)
+            scales = ring.tile([P, PASSES * P], U8, name="h_scales", align_bytes=64)
+            nc.vector.quantize_mx(codes[:].bitcast(FP8X4), scales[:], turned[j][:])
+            quantised[j] = (codes, scales)
+
+        groups = [[0, 1, 2, 3], [4, 5, 6, 7], [8, 9, 10], [11]]
+        place = {j: (g, k) for g, members in enumerate(groups) for k, j in enumerate(members)}
+        y_slots = keep.tile([P, S], F32, name="y_slots")
+
+        def second_layer(j):
+            g, k = place[j]
+            if k == 0:
+                y_bank[g] = psum.tile([P, PASS], F32, name="y", bufs=2)
+            codes, scales = quantised[j]
+            e = tiles[j][2]
+            for s in range(PASSES):
+                nc.tensor.matmul_mx(
+                    y_bank[g][:, P * k : P * (k + 1)],
+                    lhsT=w2w[:, PASSES * e + s, :].bitcast(FP4X4),
+                    lhsT_scale=w2s[:, PASSES * e + s, :],
+                    rhs=codes[:, P * s : P * (s + 1)].bitcast(FP8X4),
+                    rhs_scale=scales[:, P * s : P * (s + 1)],
+                    start=(s == 0),
+                    stop=(s == PASSES - 1),
+                )
+            if k + 1 < len(groups[g]):
+                return
+            if g == 0:
+                nc.scalar.copy(y_slots[:], y_bank[g][:])
+                return
+            width = P * len(groups[g])
+            c0 = P * (groups[g][0] - n_routed)
+            result = keep.tile([P, width], F32, name=f"result{g}")
+            nc.vector.tensor_tensor(result[:], y_bank[g][:, :width], routed[:, c0 : c0 + width], ADD)
+            nc.sync.dma_start(out[:, c0 : c0 + width], result[:])
+
+        def scatter(k):
+            cols = slice(P * k, P * (k + 1))
+            piece = offsets[:, P * k // 16 : P * (k + 1) // 16]
+            nc.vector.tensor_tensor(routed[:].indirect(piece), y_slots[:, cols], gates[:, cols], MULT)
+
+        n_tiles = len(tiles)
+        for step in range(n_tiles + 2):
+            if step < n_tiles:
+                first_layer(step)
+            if 0 <= step - 6 < n_routed:
+                scatter(step - 6)
+            if 0 <= step - 2:
+                second_layer(step - 2)
+            if 0 <= step - 1 < n_tiles:
+                turn(step - 1)
+                quantise(step - 1)

@@ -30,87 +30,111 @@ def tile_moe_shr_glu_relu_kernel(
     nc = tc.nc
     with ExitStack() as ctx:
         keep = ctx.enter_context(tc.tile_pool(name="keep", bufs=1))
-        ring = ctx.enter_context(tc.tile_pool(name="ring", bufs=3))
+        ring = ctx.enter_context(tc.tile_pool(name="ring", bufs=4))
         psum = ctx.enter_context(tc.psum_pool(name="psum", bufs=2))
 
-        def zeroed_plane(name, shape):
+        def zeroed_plane(engine, name, shape):
             plane = keep.tile(shape, U8, name=name, align_bytes=64)
-            nc.vector.memset(plane[:].bitcast(I32), 0)
+            engine.memset(plane[:].bitcast(I32), 0)
             return plane
 
-        def load_scale_rows(plane, rows):
+        def load_scale_rows(queue, plane, rows):
             for r in range(4):
-                nc.sync.dma_start(plane[r:P:32].bitcast(I32), rows[r:16:4].bitcast(I32))
+                queue.dma_start(plane[r:P:32].bitcast(I32), rows[r:16:4].bitcast(I32))
 
-        def load_words(name, src):
-            words = keep.tile([P, 2 * H], U8, name=name, align_bytes=64)
-            nc.sync.dma_start(words[:].bitcast(I32), src.bitcast(I32))
-            return words
+        def load_quadrant(plane, rows, q):
+            four = rows[4 * q : 4 * q + 4, :].bitcast(I32)
+            nc.sync.dma_start(
+                plane[32 * q : 32 * q + 32, :].bitcast(I32), four.unsqueeze(0).to_broadcast([8, 4, four.shape[1]])
+            )
 
-        xs = zeroed_plane("xs", [P, T])
-        w1s_first = zeroed_plane("w1s_first", [P, 1, H])
-        w3s_first = zeroed_plane("w3s_first", [P, 1, H])
-        w1s_rest = zeroed_plane("w1s_rest", [P, E, H])
-        w3s_rest = zeroed_plane("w3s_rest", [P, E, H])
-        w2s = zeroed_plane("w2s", [P, (E + 1) * PASSES, N])
+        def load_words(words, src):
+            nc.sync.dma_start(words.bitcast(I32), src.bitcast(I32))
+
+        w1s_routed = zeroed_plane(nc.vector, "w1s_routed", [P, E, H])
+        w3s_routed = zeroed_plane(nc.gpsimd, "w3s_routed", [P, E, H])
+        w2s = zeroed_plane(nc.gpsimd, "w2s", [P, (E + 1) * PASSES, N])
         routed = keep.tile([P, T], F32, name="routed")
         nc.vector.memset(routed[:], 0.0)
         ident = keep.tile([P, P], F32, name="ident")
         make_identity(nc, ident[:])
 
-        xw = keep.tile([P, T], I32, name="xw", align_bytes=64)
-        nc.sync.dma_start(xw[:], x_words[0].rearrange("p t r -> p (t r)").bitcast(I32))
+        xs = keep.tile([P, T], U8, name="xs", align_bytes=64)
+        w1s_shared = keep.tile([P, H], U8, name="w1s_shared", align_bytes=64)
+        w3s_shared = keep.tile([P, H], U8, name="w3s_shared", align_bytes=64)
+        w1w_shared = keep.tile([P, 2 * H], U8, name="w1w_shared", align_bytes=64)
+        w3w_shared = keep.tile([P, 2 * H], U8, name="w3w_shared", align_bytes=64)
+        w1w_routed = keep.tile([P, E, 2 * H], U8, name="w1w_routed", align_bytes=64)
+        w3w_routed = keep.tile([P, E, 2 * H], U8, name="w3w_routed", align_bytes=64)
         offsets = keep.tile([P, S // 16], U16, name="offsets")
         nc.sync.dma_start(offsets[:], offs)
-        load_scale_rows(xs, x_scales[0])
-        w1w = [load_words("w1w0", w1_words[0, 0])]
-        w3w = [load_words("w3w0", w3_words[0, 0])]
-        w1_rows = w1_scales[:, 0].rearrange("e q i -> q e i")
-        w3_rows = w3_scales[:, 0].rearrange("e q i -> q e i")
-        load_scale_rows(w1s_first, w1_rows[:, 0:1, :])
-        load_scale_rows(w3s_first, w3_rows[:, 0:1, :])
-        load_scale_rows(w1s_rest, w1_rows[:, 1:, :])
-        load_scale_rows(w3s_rest, w3_rows[:, 1:, :])
-        w1w.append(load_words("w1w1", w1_words[1, 0]))
-        w3w.append(load_words("w3w1", w3_words[1, 0]))
+        for q in range(4):
+            load_quadrant(xs, x_scales[0], q)
+        for q in range(2):
+            load_quadrant(w3s_shared, w3_scales[E, 0], q)
+        xw = keep.tile([P, T], I32, name="xw", align_bytes=64)
+        nc.sync.dma_start(xw[:], x_words[0].rearrange("p t r -> p (t r)").bitcast(I32))
+        load_words(w3w_shared[:], w3_words[E, 0])
+        for q in range(2, 4):
+            load_quadrant(w3s_shared, w3_scales[E, 0], q)
+        load_words(w1w_shared[:], w1_words[E, 0])
+        for q in range(4):
+            load_quadrant(w1s_shared, w1_scales[E, 0], q)
+        load_words(w3w_routed[:], w3_words[:E, 0].rearrange("e p c -> p e c"))
+        load_scale_rows(nc.sync, w3s_routed, w3_scales[:E, 0].rearrange("e q i -> q e i"))
+        load_words(w1w_routed[:], w1_words[:E, 0].rearrange("e p c -> p e c"))
+        load_scale_rows(nc.sync, w1s_routed, w1_scales[:E, 0].rearrange("e q i -> q e i"))
         w2w = keep.tile([P, (E + 1) * PASSES, 2 * N], U8, name="w2w", align_bytes=64)
-        nc.sync.dma_start(w2w[:].bitcast(I32), w2_words.rearrange("e s p n -> p (e s) n").bitcast(I32))
-        load_scale_rows(w2s, w2_scales.rearrange("e s q n -> q (e s) n"))
-        w1w.append(load_words("w1w2", w1_words[2, 0]))
-        w3w.append(load_words("w3w2", w3_words[2, 0]))
+        load_words(w2w[:], w2_words.rearrange("e s p n -> p (e s) n"))
+        load_scale_rows(nc.sync, w2s, w2_scales.rearrange("e s q n -> q (e s) n"))
         gates = keep.tile([P, S], F32, name="gates")
         nc.sync.dma_start(gates[:], gate)
-        w1s = [w1s_first[:, 0, :], w1s_rest[:, 0, :], w1s_rest[:, 1, :]]
-        w3s = [w3s_first[:, 0, :], w3s_rest[:, 0, :], w3s_rest[:, 1, :]]
 
-        tiles = []
-        for first, count in ((0, P), (P, P), (2 * P, 2 * P)):
-            gw = keep.tile([P, count], I32, name=f"gw{first}", align_bytes=64)
-            gs = keep.tile([P, count], U8, name=f"gs{first}", align_bytes=64)
-            piece = offsets[:, first // 16 : (first + count) // 16]
+        def regroup(name, columns, dtype):
+            grouped = keep.tile([P, H], dtype, name=name, align_bytes=64)
+            nc.vector.tensor_copy(
+                grouped[:].rearrange("p (g d m) -> p g d m", m=P, d=4),
+                columns.rearrange("p (g m d) -> p g d m", m=P, d=4),
+            )
+            return grouped
+
+        w3_grouped = (regroup("w3w_grouped", w3w_shared[:].bitcast(U16), U16), regroup("w3s_grouped", w3s_shared[:], U8))
+        w1_grouped = (regroup("w1w_grouped", w1w_shared[:].bitcast(U16), U16), regroup("w1s_grouped", w1s_shared[:], U8))
+
+        gathered = []
+        for e in range(E):
+            gw = keep.tile([P, C], I32, name=f"gw{e}", align_bytes=64)
+            gs = keep.tile([P, C], U8, name=f"gs{e}", align_bytes=64)
+            piece = offsets[:, C * e // 16 : C * (e + 1) // 16]
             nc.vector.tensor_copy(gw[:].bitcast(U32), xw[:].bitcast(U32).indirect(piece))
             nc.vector.tensor_copy(gs[:], xs[:].indirect(piece))
-            for c in range(0, count, P):
-                tiles.append((gw[:, c : c + P], gs[:, c : c + P], (first + c) // C))
-        n_routed = len(tiles)
-        for c in range(0, T, P):
-            tiles.append((xw[:, c : c + P], xs[:, c : c + P], E))
+            gathered.append((gw, gs))
 
-        def order(ap):
-            return ap.rearrange("t (p u e) -> t u p e", u=2, e=2)
-
-        def plain(ap):
-            return ap.rearrange("t (u p e) -> t u p e", u=2, e=2)
-
+        tiles = [("s", 0), ("s", 1), ("r", 0), ("s", 2), ("r", 1), ("r", 2), ("s", 3), ("r", 3)]
+        tiles = tiles + [("s", k) for k in range(4, 8)]
+        batches = [tiles[0:2], tiles[2:4], tiles[4:6], tiles[6:8], tiles[8:10], tiles[10:11], tiles[11:12]]
+        batch_of = {j: (g, k) for g, members in enumerate(batches) for k, j in enumerate(members)}
         hidden, turned, quantised, y_bank = {}, {}, {}, {}
 
-        def first_layer(j):
-            words, scales, e = tiles[j]
+        def hidden_rows(j):
+            g, k = batch_of[j]
+            if g not in turned:
+                turned[g] = ring.tile([P, len(batches[g]) * H], BF16, name="ht", align_bytes=64, bufs=3)
+            return turned[g][:, H * k : H * (k + 1)]
+
+        def gated_product(h, a, b, read, write):
+            relu_a = ring.tile([P, PASS], F32, name="relu_a")
+            nc.scalar.activation(write(relu_a[:]), read(a), RELU)
+            nc.vector.tensor_tensor(write(h), read(b), write(relu_a[:]), MULT)
+
+        def first_layer_routed(j):
+            e, c = divmod(P * j[1], C)
+            words, scales = gathered[e][0][:, c : c + P], gathered[e][1][:, c : c + P]
             h = ring.tile([P, PASSES, PASS], BF16, name="h", align_bytes=64)
             for s in range(PASSES):
                 a = psum.tile([P, PASS], F32, name="a", bufs=2)
                 b = psum.tile([P, PASS], F32, name="b", bufs=3)
-                for acc, ww, ws in ((a, w1w[e], w1s[e]), (b, w3w[e], w3s[e])):
+                for acc, ww, ws in ((b, w3w_routed[:, e], w3s_routed[:, e]), (a, w1w_routed[:, e], w1s_routed[:, e])):
                     nc.tensor.matmul_mx(
                         acc[:],
                         lhsT=words.bitcast(FP8X4),
@@ -120,41 +144,78 @@ def tile_moe_shr_glu_relu_kernel(
                         start=True,
                         stop=True,
                     )
-                relu_a = ring.tile([P, PASS], F32, name="relu_a")
-                nc.scalar.activation(plain(relu_a[:]), order(a[:]), RELU)
-                nc.vector.tensor_tensor(plain(h[:, s, :]), order(b[:]), plain(relu_a[:]), MULT)
+                gated_product(
+                    h[:, s, :],
+                    a[:],
+                    b[:],
+                    lambda ap: ap.rearrange("t (p u e) -> t u p e", u=2, e=2),
+                    lambda ap: ap.rearrange("t (u p e) -> t u p e", u=2, e=2),
+                )
             hidden[j] = h
+
+        def first_layer_shared(j):
+            words, scales = xw[:, P * j[1] : P * (j[1] + 1)], xs[:, P * j[1] : P * (j[1] + 1)]
+            ht = hidden_rows(j)
+            for s in range(PASSES):
+                a = psum.tile([P, PASS], F32, name="a", bufs=2)
+                b = psum.tile([P, PASS], F32, name="b", bufs=3)
+                for acc, (ww, ws) in ((b, w3_grouped), (a, w1_grouped)):
+                    for d in range(4):
+                        cols = slice(PASS * s + P * d, PASS * s + P * (d + 1))
+                        nc.tensor.matmul_mx(
+                            acc[:, P * d : P * (d + 1)],
+                            lhsT=ww[:, cols].bitcast(FP4X4),
+                            lhsT_scale=ws[:, cols],
+                            rhs=words.bitcast(FP8X4),
+                            rhs_scale=scales,
+                            start=True,
+                            stop=True,
+                        )
+                gated_product(
+                    ht[:, PASS * s : PASS * (s + 1)],
+                    a[:],
+                    b[:],
+                    lambda ap: ap.rearrange("p (d t) -> p t d", d=4),
+                    lambda ap: ap.rearrange("p (t d) -> p t d", d=4),
+                )
 
         def turn(j):
             h = hidden[j]
-            t_ps = psum.tile([P, PASSES * 2, P], F32, name="t_ps", bufs=1)
+            t_ps = psum.tile([P, PASS], F32, name="t_ps", tag="turn", bufs=1)
             for s in range(PASSES):
                 pairs = h[:, s, :].bitcast(F32)
                 for u in range(2):
-                    nc.tensor.transpose(t_ps[:, 2 * s + u, :], pairs[:, P * u : P * (u + 1)], ident[:])
-            ht = ring.tile([P, PASSES * PASS], BF16, name="ht", align_bytes=64)
+                    nc.tensor.transpose(
+                        t_ps[:, P * (2 * s + u) : P * (2 * s + u + 1)], pairs[:, P * u : P * (u + 1)], ident[:]
+                    )
             nc.scalar.copy(
-                ht[:].bitcast(F32).rearrange("p (s t u) -> p s t u", s=PASSES, u=2),
-                t_ps[:].rearrange("p (s u) t -> p s t u", u=2),
+                hidden_rows(j).bitcast(F32).rearrange("p (s t u) -> p s t u", s=PASSES, u=2),
+                t_ps[:].rearrange("p (s u t) -> p s t u", s=PASSES, u=2),
             )
-            turned[j] = ht
 
-        def quantise(j):
-            codes = ring.tile([P, PASSES * P], U32, name="codes", align_bytes=64)
-            scales = ring.tile([P, PASSES * P], U8, name="h_scales", align_bytes=64)
-            nc.vector.quantize_mx(codes[:].bitcast(FP8X4), scales[:], turned[j][:])
-            quantised[j] = (codes, scales)
+        def quantise(g):
+            width = len(batches[g]) * PASSES * P
+            codes = ring.tile([P, width], U32, name="codes", align_bytes=64, bufs=3)
+            scales = ring.tile([P, width], U8, name="h_scales", align_bytes=64, bufs=3)
+            nc.vector.quantize_mx(codes[:].bitcast(FP8X4), scales[:], turned[g][:])
+            for k, j in enumerate(batches[g]):
+                cols = slice(PASSES * P * k, PASSES * P * (k + 1))
+                quantised[j] = (codes[:, cols], scales[:, cols])
 
-        groups = [[0, 1, 2, 3], [4, 5, 6, 7], [8, 9, 10], [11]]
-        place = {j: (g, k) for g, members in enumerate(groups) for k, j in enumerate(members)}
-        y_slots = keep.tile([P, S], F32, name="y_slots")
+        groups = [
+            ([("s", k) for k in range(0, 4)], "early"),
+            ([("r", k) for k in range(0, 4)], "late"),
+            ([("s", k) for k in range(4, 7)], "late"),
+            ([("s", 7)], "turn"),
+        ]
+        place = {j: (g, k) for g, (members, tag) in enumerate(groups) for k, j in enumerate(members)}
 
         def second_layer(j):
             g, k = place[j]
             if k == 0:
-                y_bank[g] = psum.tile([P, PASS], F32, name="y", bufs=2)
+                y_bank[g] = psum.tile([P, PASS], F32, name="y", tag=groups[g][1], bufs=1)
             codes, scales = quantised[j]
-            e = tiles[j][2]
+            e = E if j[0] == "s" else P * j[1] // C
             for s in range(PASSES):
                 nc.tensor.matmul_mx(
                     y_bank[g][:, P * k : P * (k + 1)],
@@ -165,30 +226,45 @@ def tile_moe_shr_glu_relu_kernel(
                     start=(s == 0),
                     stop=(s == PASSES - 1),
                 )
-            if k + 1 < len(groups[g]):
-                return
-            if g == 0:
-                nc.scalar.copy(y_slots[:], y_bank[g][:])
-                return
-            width = P * len(groups[g])
-            c0 = P * (groups[g][0] - n_routed)
+
+        def scatter(e):
+            cols = slice(C * e, C * (e + 1))
+            y_slots = keep.tile([P, C], F32, name=f"y_slots{e}")
+            nc.scalar.copy(y_slots[:], y_bank[1][:, cols])
+            piece = offsets[:, C * e // 16 : C * (e + 1) // 16]
+            nc.vector.tensor_tensor(routed[:].indirect(piece), y_slots[:], gates[:, cols], MULT)
+
+        def finish(g):
+            members = groups[g][0]
+            width = P * len(members)
+            c0 = P * members[0][1]
             result = keep.tile([P, width], F32, name=f"result{g}")
             nc.vector.tensor_tensor(result[:], y_bank[g][:, :width], routed[:, c0 : c0 + width], ADD)
             nc.sync.dma_start(out[:, c0 : c0 + width], result[:])
 
-        def scatter(k):
-            cols = slice(P * k, P * (k + 1))
-            piece = offsets[:, P * k // 16 : P * (k + 1) // 16]
-            nc.vector.tensor_tensor(routed[:].indirect(piece), y_slots[:, cols], gates[:, cols], MULT)
-
         n_tiles = len(tiles)
         for step in range(n_tiles + 2):
             if step < n_tiles:
-                first_layer(step)
-            if 0 <= step - 6 < n_routed:
-                scatter(step - 6)
-            if 0 <= step - 2:
-                second_layer(step - 2)
+                if tiles[step][0] == "r":
+                    first_layer_routed(tiles[step])
+                else:
+                    first_layer_shared(tiles[step])
+            for members in batches:
+                if 0 <= step - 2 and members[-1] == tiles[step - 2]:
+                    for j in members:
+                        second_layer(j)
+                        if j == ("r", 2):
+                            scatter(0)
+                        if j == ("r", 3):
+                            scatter(1)
+                            finish(0)
+                        if j == ("s", 6):
+                            finish(2)
+                        if j == ("s", 7):
+                            finish(3)
             if 0 <= step - 1 < n_tiles:
-                turn(step - 1)
-                quantise(step - 1)
+                if tiles[step - 1][0] == "r":
+                    turn(tiles[step - 1])
+                for g, members in enumerate(batches):
+                    if members[-1] == tiles[step - 1]:
+                        quantise(g)

@@ -67,39 +67,45 @@ def tile_moe_shr_glu_relu_kernel(
         w1w_routed = keep.tile([P, E, 2 * H], U8, name="w1w_routed", align_bytes=64)
         w3w_routed = keep.tile([P, E, 2 * H], U8, name="w3w_routed", align_bytes=64)
         offsets = keep.tile([P, S // 16], U16, name="offsets")
-        nc.sync.dma_start(offsets[:], offs)
-        for q in range(4):
-            load_quadrant(xs, x_scales[0], q)
-        for q in range(2):
-            load_quadrant(w3s_shared, w3_scales[E, 0], q)
         xw = keep.tile([P, T], I32, name="xw", align_bytes=64)
-        nc.sync.dma_start(xw[:], x_words[0].rearrange("p t r -> p (t r)").bitcast(I32))
-        load_words(w3w_shared[:], w3_words[E, 0])
-        for q in range(2, 4):
-            load_quadrant(w3s_shared, w3_scales[E, 0], q)
-        load_words(w1w_shared[:], w1_words[E, 0])
         for q in range(4):
             load_quadrant(w1s_shared, w1_scales[E, 0], q)
-        load_words(w3w_routed[:], w3_words[:E, 0].rearrange("e p c -> p e c"))
-        load_scale_rows(nc.sync, w3s_routed, w3_scales[:E, 0].rearrange("e q i -> q e i"))
+        load_words(w1w_shared[:], w1_words[E, 0])
+        nc.sync.dma_start(offsets[:], offs)
+        load_quadrant(xs, x_scales[0], 0)
+        nc.sync.dma_start(xw[:], x_words[0].rearrange("p t r -> p (t r)").bitcast(I32))
+        for q in range(1, 4):
+            load_quadrant(xs, x_scales[0], q)
+        for q in range(4):
+            load_quadrant(w3s_shared, w3_scales[E, 0], q)
+        load_words(w3w_shared[:], w3_words[E, 0])
         load_words(w1w_routed[:], w1_words[:E, 0].rearrange("e p c -> p e c"))
         load_scale_rows(nc.sync, w1s_routed, w1_scales[:E, 0].rearrange("e q i -> q e i"))
+        load_words(w3w_routed[:], w3_words[:E, 0].rearrange("e p c -> p e c"))
+        load_scale_rows(nc.sync, w3s_routed, w3_scales[:E, 0].rearrange("e q i -> q e i"))
         w2w = keep.tile([P, (E + 1) * PASSES, 2 * N], U8, name="w2w", align_bytes=64)
         load_words(w2w[:], w2_words.rearrange("e s p n -> p (e s) n"))
         load_scale_rows(nc.sync, w2s, w2_scales.rearrange("e s q n -> q (e s) n"))
         gates = keep.tile([P, S], F32, name="gates")
         nc.sync.dma_start(gates[:], gate)
 
-        def regroup(name, columns, dtype):
-            grouped = keep.tile([P, H], dtype, name=name, align_bytes=64)
+        def regroup(name, columns):
+            grouped = keep.tile(list(columns.shape), columns.dtype, name=name, align_bytes=64)
             nc.vector.tensor_copy(
                 grouped[:].rearrange("p (g d m) -> p g d m", m=P, d=4),
                 columns.rearrange("p (g m d) -> p g d m", m=P, d=4),
             )
             return grouped
 
-        w3_grouped = (regroup("w3w_grouped", w3w_shared[:].bitcast(U16), U16), regroup("w3s_grouped", w3s_shared[:], U8))
-        w1_grouped = (regroup("w1w_grouped", w1w_shared[:].bitcast(U16), U16), regroup("w1s_grouped", w1s_shared[:], U8))
+        w1s_grouped = regroup("w1s_grouped", w1s_shared[:])
+        w1w_grouped = regroup("w1w_grouped", w1w_shared[:].bitcast(U16))
+        w1_grouped, w3_grouped = [], []
+        for s in range(PASSES):
+            cols = slice(PASS * s, PASS * (s + 1))
+            w1_grouped.append((w1w_grouped[:, cols], w1s_grouped[:, cols]))
+            scales = regroup(f"w3s_grouped{s}", w3s_shared[:, cols])
+            words = regroup(f"w3w_grouped{s}", w3w_shared[:].bitcast(U16)[:, cols])
+            w3_grouped.append((words[:], scales[:]))
 
         gathered = []
         for e in range(E):
@@ -110,31 +116,36 @@ def tile_moe_shr_glu_relu_kernel(
             nc.vector.tensor_copy(gs[:], xs[:].indirect(piece))
             gathered.append((gw, gs))
 
-        tiles = [("s", 0), ("s", 1), ("r", 0), ("s", 2), ("r", 1), ("r", 2), ("s", 3), ("r", 3)]
-        tiles = tiles + [("s", k) for k in range(4, 8)]
-        batches = [tiles[0:2], tiles[2:4], tiles[4:6], tiles[6:8], tiles[8:10], tiles[10:11], tiles[11:12]]
-        batch_of = {j: (g, k) for g, members in enumerate(batches) for k, j in enumerate(members)}
+        tiles = [("s", k) for k in range(4)] + [("r", k) for k in range(4)] + [("s", k) for k in range(4, 8)]
+        units = [(j, s) for j in tiles for s in range(PASSES)]
+        batches = [units[0:4], units[4:8], units[8:12], units[12:16], units[16:20], units[20:22], units[22:23], units[23:24]]
+        batch_of = {unit: (g, k) for g, members in enumerate(batches) for k, unit in enumerate(members)}
         hidden, turned, quantised, y_bank = {}, {}, {}, {}
 
-        def hidden_rows(j):
-            g, k = batch_of[j]
+        def hidden_rows(unit, count):
+            g, k = batch_of[unit]
             if g not in turned:
-                turned[g] = ring.tile([P, len(batches[g]) * H], BF16, name="ht", align_bytes=64, bufs=3)
-            return turned[g][:, H * k : H * (k + 1)]
+                turned[g] = ring.tile([P, len(batches[g]) * PASS], BF16, name="ht", align_bytes=64, bufs=4)
+            return turned[g][:, PASS * k : PASS * (k + count)]
 
-        def gated_product(h, a, b, read, write):
-            relu_a = ring.tile([P, PASS], F32, name="relu_a")
+        def gated_product(unit, h, a, b, read, write):
+            relu_a = ring.tile([P, PASS], F32, name="relu_a", bufs=6)
             nc.scalar.activation(write(relu_a[:]), read(a), RELU)
             nc.vector.tensor_tensor(write(h), read(b), write(relu_a[:]), MULT)
+
+        def in_order(unit, for_a, for_b):
+            return (for_a, for_b) if unit == units[0] else (for_b, for_a)
 
         def first_layer_routed(j):
             e, c = divmod(P * j[1], C)
             words, scales = gathered[e][0][:, c : c + P], gathered[e][1][:, c : c + P]
             h = ring.tile([P, PASSES, PASS], BF16, name="h", align_bytes=64)
             for s in range(PASSES):
-                a = psum.tile([P, PASS], F32, name="a", bufs=2)
+                a = psum.tile([P, PASS], F32, name="a", bufs=3)
                 b = psum.tile([P, PASS], F32, name="b", bufs=3)
-                for acc, ww, ws in ((b, w3w_routed[:, e], w3s_routed[:, e]), (a, w1w_routed[:, e], w1s_routed[:, e])):
+                for acc, ww, ws in in_order(
+                    (j, s), (a, w1w_routed[:, e], w1s_routed[:, e]), (b, w3w_routed[:, e], w3s_routed[:, e])
+                ):
                     nc.tensor.matmul_mx(
                         acc[:],
                         lhsT=words.bitcast(FP8X4),
@@ -145,6 +156,7 @@ def tile_moe_shr_glu_relu_kernel(
                         stop=True,
                     )
                 gated_product(
+                    (j, s),
                     h[:, s, :],
                     a[:],
                     b[:],
@@ -155,13 +167,12 @@ def tile_moe_shr_glu_relu_kernel(
 
         def first_layer_shared(j):
             words, scales = xw[:, P * j[1] : P * (j[1] + 1)], xs[:, P * j[1] : P * (j[1] + 1)]
-            ht = hidden_rows(j)
             for s in range(PASSES):
-                a = psum.tile([P, PASS], F32, name="a", bufs=2)
+                a = psum.tile([P, PASS], F32, name="a", bufs=3)
                 b = psum.tile([P, PASS], F32, name="b", bufs=3)
-                for acc, (ww, ws) in ((b, w3_grouped), (a, w1_grouped)):
+                for acc, (ww, ws) in in_order((j, s), (a, w1_grouped[s]), (b, w3_grouped[s])):
                     for d in range(4):
-                        cols = slice(PASS * s + P * d, PASS * s + P * (d + 1))
+                        cols = slice(P * d, P * (d + 1))
                         nc.tensor.matmul_mx(
                             acc[:, P * d : P * (d + 1)],
                             lhsT=ww[:, cols].bitcast(FP4X4),
@@ -172,7 +183,8 @@ def tile_moe_shr_glu_relu_kernel(
                             stop=True,
                         )
                 gated_product(
-                    ht[:, PASS * s : PASS * (s + 1)],
+                    (j, s),
+                    hidden_rows((j, s), 1),
                     a[:],
                     b[:],
                     lambda ap: ap.rearrange("p (d t) -> p t d", d=4),
@@ -189,23 +201,22 @@ def tile_moe_shr_glu_relu_kernel(
                         t_ps[:, P * (2 * s + u) : P * (2 * s + u + 1)], pairs[:, P * u : P * (u + 1)], ident[:]
                     )
             nc.scalar.copy(
-                hidden_rows(j).bitcast(F32).rearrange("p (s t u) -> p s t u", s=PASSES, u=2),
+                hidden_rows((j, 0), PASSES).bitcast(F32).rearrange("p (s t u) -> p s t u", s=PASSES, u=2),
                 t_ps[:].rearrange("p (s u t) -> p s t u", s=PASSES, u=2),
             )
 
         def quantise(g):
-            width = len(batches[g]) * PASSES * P
+            width = len(batches[g]) * P
             codes = ring.tile([P, width], U32, name="codes", align_bytes=64, bufs=3)
             scales = ring.tile([P, width], U8, name="h_scales", align_bytes=64, bufs=3)
             nc.vector.quantize_mx(codes[:].bitcast(FP8X4), scales[:], turned[g][:])
-            for k, j in enumerate(batches[g]):
-                cols = slice(PASSES * P * k, PASSES * P * (k + 1))
-                quantised[j] = (codes[:, cols], scales[:, cols])
+            for k, unit in enumerate(batches[g]):
+                quantised[unit] = (codes[:, P * k : P * (k + 1)], scales[:, P * k : P * (k + 1)])
 
         groups = [
-            ([("s", k) for k in range(0, 4)], "early"),
-            ([("r", k) for k in range(0, 4)], "late"),
-            ([("s", k) for k in range(4, 7)], "late"),
+            ([("s", k) for k in range(0, 4)], "y"),
+            ([("r", k) for k in range(0, 4)], "y"),
+            ([("s", k) for k in range(4, 7)], "y"),
             ([("s", 7)], "turn"),
         ]
         place = {j: (g, k) for g, (members, tag) in enumerate(groups) for k, j in enumerate(members)}
@@ -214,15 +225,15 @@ def tile_moe_shr_glu_relu_kernel(
             g, k = place[j]
             if k == 0:
                 y_bank[g] = psum.tile([P, PASS], F32, name="y", tag=groups[g][1], bufs=1)
-            codes, scales = quantised[j]
             e = E if j[0] == "s" else P * j[1] // C
             for s in range(PASSES):
+                codes, scales = quantised[(j, s)]
                 nc.tensor.matmul_mx(
                     y_bank[g][:, P * k : P * (k + 1)],
                     lhsT=w2w[:, PASSES * e + s, :].bitcast(FP4X4),
                     lhsT_scale=w2s[:, PASSES * e + s, :],
-                    rhs=codes[:, P * s : P * (s + 1)].bitcast(FP8X4),
-                    rhs_scale=scales[:, P * s : P * (s + 1)],
+                    rhs=codes.bitcast(FP8X4),
+                    rhs_scale=scales,
                     start=(s == 0),
                     stop=(s == PASSES - 1),
                 )
@@ -239,32 +250,37 @@ def tile_moe_shr_glu_relu_kernel(
             width = P * len(members)
             c0 = P * members[0][1]
             result = keep.tile([P, width], F32, name=f"result{g}")
-            nc.vector.tensor_tensor(result[:], y_bank[g][:, :width], routed[:, c0 : c0 + width], ADD)
+            shared_part = early[:] if g == 0 else y_bank[g][:, :width]
+            nc.vector.tensor_tensor(result[:], shared_part, routed[:, c0 : c0 + width], ADD)
             nc.sync.dma_start(out[:, c0 : c0 + width], result[:])
 
+        early = keep.tile([P, PASS], F32, name="early")
         n_tiles = len(tiles)
+        done = []
         for step in range(n_tiles + 2):
             if step < n_tiles:
                 if tiles[step][0] == "r":
                     first_layer_routed(tiles[step])
                 else:
                     first_layer_shared(tiles[step])
-            for members in batches:
-                if 0 <= step - 2 and members[-1] == tiles[step - 2]:
-                    for j in members:
-                        second_layer(j)
-                        if j == ("r", 2):
-                            scatter(0)
-                        if j == ("r", 3):
-                            scatter(1)
-                            finish(0)
-                        if j == ("s", 6):
-                            finish(2)
-                        if j == ("s", 7):
-                            finish(3)
+            for j in tiles:
+                if j not in done and (j, PASSES - 1) in quantised:
+                    done.append(j)
+                    second_layer(j)
+                    if j == ("s", 3):
+                        nc.scalar.copy(early[:], y_bank[0][:])
+                    if j == ("r", 1):
+                        scatter(0)
+                    if j == ("r", 3):
+                        scatter(1)
+                        finish(0)
+                    if j == ("s", 6):
+                        finish(2)
+                    if j == ("s", 7):
+                        finish(3)
             if 0 <= step - 1 < n_tiles:
                 if tiles[step - 1][0] == "r":
                     turn(tiles[step - 1])
                 for g, members in enumerate(batches):
-                    if members[-1] == tiles[step - 1]:
+                    if members[-1][0] == tiles[step - 1]:
                         quantise(g)

@@ -38,85 +38,68 @@ def tile_moe_shr_glu_relu_kernel(
             engine.memset(plane[:].bitcast(I32), 0)
             return plane
 
-        def load_scale_rows(queue, plane, rows):
-            for r in range(4):
-                queue.dma_start(plane[r:P:32].bitcast(I32), rows[r:16:4].bitcast(I32))
-
-        def load_quadrant(plane, rows, q):
-            four = rows[4 * q : 4 * q + 4, :].bitcast(I32)
-            nc.sync.dma_start(
-                plane[32 * q : 32 * q + 32, :].bitcast(I32), four.unsqueeze(0).to_broadcast([8, 4, four.shape[1]])
-            )
+        def load_scale_rows(plane, rows, which):
+            for r in which:
+                nc.sync.dma_start(plane[r:P:32].bitcast(I32), rows[r:16:4].bitcast(I32))
 
         def load_words(words, src):
             nc.sync.dma_start(words.bitcast(I32), src.bitcast(I32))
 
-        w1s_routed = zeroed_plane(nc.vector, "w1s_routed", [P, E, H])
-        w3s_routed = zeroed_plane(nc.gpsimd, "w3s_routed", [P, E, H])
+        w1s = zeroed_plane(nc.gpsimd, "w1s", [P, E + 1, H])
+        xs = zeroed_plane(nc.vector, "xs", [P, T])
+        w3s = zeroed_plane(nc.vector, "w3s", [P, E + 1, H])
         w2s = zeroed_plane(nc.gpsimd, "w2s", [P, (E + 1) * PASSES, N])
         routed = keep.tile([P, T], F32, name="routed")
         nc.vector.memset(routed[:], 0.0)
         ident = keep.tile([P, P], F32, name="ident")
         make_identity(nc, ident[:])
 
-        xs = keep.tile([P, T], U8, name="xs", align_bytes=64)
-        w1s_shared = keep.tile([P, H], U8, name="w1s_shared", align_bytes=64)
-        w3s_shared = keep.tile([P, H], U8, name="w3s_shared", align_bytes=64)
         w1w_shared = keep.tile([P, 2 * H], U8, name="w1w_shared", align_bytes=64)
         w3w_shared = keep.tile([P, 2 * H], U8, name="w3w_shared", align_bytes=64)
         w1w_routed = keep.tile([P, E, 2 * H], U8, name="w1w_routed", align_bytes=64)
         w3w_routed = keep.tile([P, E, 2 * H], U8, name="w3w_routed", align_bytes=64)
         offsets = keep.tile([P, S // 16], U16, name="offsets")
         xw = keep.tile([P, T], I32, name="xw", align_bytes=64)
-        for q in range(4):
-            load_quadrant(w1s_shared, w1_scales[E, 0], q)
         load_words(w1w_shared[:], w1_words[E, 0])
+        load_scale_rows(w1s, w1_scales[:, 0].rearrange("e q i -> q e i"), range(4))
         nc.sync.dma_start(offsets[:], offs)
-        load_quadrant(xs, x_scales[0], 0)
+        load_scale_rows(xs, x_scales[0], range(1))
         nc.sync.dma_start(xw[:], x_words[0].rearrange("p t r -> p (t r)").bitcast(I32))
-        for q in range(1, 4):
-            load_quadrant(xs, x_scales[0], q)
-        for q in range(4):
-            load_quadrant(w3s_shared, w3_scales[E, 0], q)
+        load_scale_rows(xs, x_scales[0], range(1, 4))
         load_words(w3w_shared[:], w3_words[E, 0])
+        load_scale_rows(w3s, w3_scales[:, 0].rearrange("e q i -> q e i"), range(4))
         load_words(w1w_routed[:], w1_words[:E, 0].rearrange("e p c -> p e c"))
-        load_scale_rows(nc.sync, w1s_routed, w1_scales[:E, 0].rearrange("e q i -> q e i"))
         load_words(w3w_routed[:], w3_words[:E, 0].rearrange("e p c -> p e c"))
-        load_scale_rows(nc.sync, w3s_routed, w3_scales[:E, 0].rearrange("e q i -> q e i"))
         w2w = keep.tile([P, (E + 1) * PASSES, 2 * N], U8, name="w2w", align_bytes=64)
         load_words(w2w[:], w2_words.rearrange("e s p n -> p (e s) n"))
-        load_scale_rows(nc.sync, w2s, w2_scales.rearrange("e s q n -> q (e s) n"))
+        load_scale_rows(w2s, w2_scales.rearrange("e s q n -> q (e s) n"), range(4))
         gates = keep.tile([P, S], F32, name="gates")
         nc.sync.dma_start(gates[:], gate)
 
-        def regroup(name, columns):
+        def regroup(name, columns, run):
             grouped = keep.tile(list(columns.shape), columns.dtype, name=name, align_bytes=64)
             nc.vector.tensor_copy(
-                grouped[:].rearrange("p (g d m) -> p g d m", m=P, d=4),
-                columns.rearrange("p (g m d) -> p g d m", m=P, d=4),
+                grouped[:].rearrange("p (g d b m) -> p g b d m", d=4, b=P // run, m=run),
+                columns.rearrange("p (g b m d) -> p g b d m", d=4, b=P // run, m=run),
             )
             return grouped
 
-        w1s_grouped = regroup("w1s_grouped", w1s_shared[:])
-        w1w_grouped = regroup("w1w_grouped", w1w_shared[:].bitcast(U16))
+        w1s_grouped = regroup("w1s_grouped", w1s[:, E], 16)
+        w1w_grouped = regroup("w1w_grouped", w1w_shared[:].bitcast(U16), 8)
         w1_grouped, w3_grouped = [], []
         for s in range(PASSES):
             cols = slice(PASS * s, PASS * (s + 1))
             w1_grouped.append((w1w_grouped[:, cols], w1s_grouped[:, cols]))
-            scales = regroup(f"w3s_grouped{s}", w3s_shared[:, cols])
-            words = regroup(f"w3w_grouped{s}", w3w_shared[:].bitcast(U16)[:, cols])
+            words = regroup(f"w3w_grouped{s}", w3w_shared[:].bitcast(U16)[:, cols], 8)
+            scales = regroup(f"w3s_grouped{s}", w3s[:, E, cols], 16)
             w3_grouped.append((words[:], scales[:]))
 
-        gathered = []
-        for e in range(E):
-            gw = keep.tile([P, C], I32, name=f"gw{e}", align_bytes=64)
-            gs = keep.tile([P, C], U8, name=f"gs{e}", align_bytes=64)
-            piece = offsets[:, C * e // 16 : C * (e + 1) // 16]
-            nc.vector.tensor_copy(gw[:].bitcast(U32), xw[:].bitcast(U32).indirect(piece))
-            nc.vector.tensor_copy(gs[:], xs[:].indirect(piece))
-            gathered.append((gw, gs))
+        gw = keep.tile([P, S], I32, name="gw", align_bytes=64)
+        gs = keep.tile([P, S], U8, name="gs", align_bytes=64)
+        nc.vector.tensor_copy(gw[:].bitcast(U32), xw[:].bitcast(U32).indirect(offsets[:]))
+        nc.vector.tensor_copy(gs[:], xs[:].indirect(offsets[:]))
 
-        tiles = [("s", k) for k in range(4)] + [("r", k) for k in range(4)] + [("s", k) for k in range(4, 8)]
+        tiles = [("s", k) for k in range(2)] + [("r", k) for k in range(4)] + [("s", k) for k in range(2, 8)]
         units = [(j, s) for j in tiles for s in range(PASSES)]
         batches = [units[0:4], units[4:8], units[8:12], units[12:16], units[16:20], units[20:22], units[22:23], units[23:24]]
         batch_of = {unit: (g, k) for g, members in enumerate(batches) for k, unit in enumerate(members)}
@@ -125,11 +108,11 @@ def tile_moe_shr_glu_relu_kernel(
         def hidden_rows(unit, count):
             g, k = batch_of[unit]
             if g not in turned:
-                turned[g] = ring.tile([P, len(batches[g]) * PASS], BF16, name="ht", align_bytes=64, bufs=4)
+                turned[g] = ring.tile([P, len(batches[g]) * PASS], BF16, name="ht", align_bytes=64, bufs=len(batches))
             return turned[g][:, PASS * k : PASS * (k + count)]
 
         def gated_product(unit, h, a, b, read, write):
-            relu_a = ring.tile([P, PASS], F32, name="relu_a", bufs=6)
+            relu_a = ring.tile([P, PASS], F32, name="relu_a", bufs=len(units))
             nc.scalar.activation(write(relu_a[:]), read(a), RELU)
             nc.vector.tensor_tensor(write(h), read(b), write(relu_a[:]), MULT)
 
@@ -137,14 +120,15 @@ def tile_moe_shr_glu_relu_kernel(
             return (for_a, for_b) if unit == units[0] else (for_b, for_a)
 
         def first_layer_routed(j):
-            e, c = divmod(P * j[1], C)
-            words, scales = gathered[e][0][:, c : c + P], gathered[e][1][:, c : c + P]
+            c = P * j[1]
+            e = c // C
+            words, scales = gw[:, c : c + P], gs[:, c : c + P]
             h = ring.tile([P, PASSES, PASS], BF16, name="h", align_bytes=64)
             for s in range(PASSES):
                 a = psum.tile([P, PASS], F32, name="a", bufs=3)
                 b = psum.tile([P, PASS], F32, name="b", bufs=3)
                 for acc, ww, ws in in_order(
-                    (j, s), (a, w1w_routed[:, e], w1s_routed[:, e]), (b, w3w_routed[:, e], w3s_routed[:, e])
+                    (j, s), (a, w1w_routed[:, e], w1s[:, e]), (b, w3w_routed[:, e], w3s[:, e])
                 ):
                     nc.tensor.matmul_mx(
                         acc[:],
@@ -207,17 +191,18 @@ def tile_moe_shr_glu_relu_kernel(
 
         def quantise(g):
             width = len(batches[g]) * P
-            codes = ring.tile([P, width], U32, name="codes", align_bytes=64, bufs=3)
-            scales = ring.tile([P, width], U8, name="h_scales", align_bytes=64, bufs=3)
+            codes = ring.tile([P, width], U32, name="codes", align_bytes=64, bufs=len(batches))
+            scales = ring.tile([P, width], U8, name="h_scales", align_bytes=64, bufs=len(batches))
             nc.vector.quantize_mx(codes[:].bitcast(FP8X4), scales[:], turned[g][:])
             for k, unit in enumerate(batches[g]):
                 quantised[unit] = (codes[:, P * k : P * (k + 1)], scales[:, P * k : P * (k + 1)])
 
         groups = [
-            ([("s", k) for k in range(0, 4)], "y"),
+            ([("s", k) for k in range(0, 2)], "y"),
             ([("r", k) for k in range(0, 4)], "y"),
-            ([("s", k) for k in range(4, 7)], "y"),
-            ([("s", 7)], "turn"),
+            ([("s", k) for k in range(2, 6)], "y"),
+            ([("s", 6)], "turn"),
+            ([("s", 7)], "y"),
         ]
         place = {j: (g, k) for g, (members, tag) in enumerate(groups) for k, j in enumerate(members)}
 
@@ -254,7 +239,7 @@ def tile_moe_shr_glu_relu_kernel(
             nc.vector.tensor_tensor(result[:], shared_part, routed[:, c0 : c0 + width], ADD)
             nc.sync.dma_start(out[:, c0 : c0 + width], result[:])
 
-        early = keep.tile([P, PASS], F32, name="early")
+        early = keep.tile([P, 2 * P], F32, name="early")
         n_tiles = len(tiles)
         done = []
         for step in range(n_tiles + 2):
@@ -267,17 +252,19 @@ def tile_moe_shr_glu_relu_kernel(
                 if j not in done and (j, PASSES - 1) in quantised:
                     done.append(j)
                     second_layer(j)
-                    if j == ("s", 3):
-                        nc.scalar.copy(early[:], y_bank[0][:])
+                    if j == ("s", 1):
+                        nc.scalar.copy(early[:], y_bank[0][:, : 2 * P])
                     if j == ("r", 1):
                         scatter(0)
                     if j == ("r", 3):
                         scatter(1)
                         finish(0)
-                    if j == ("s", 6):
+                    if j == ("s", 5):
                         finish(2)
-                    if j == ("s", 7):
+                    if j == ("s", 6):
                         finish(3)
+                    if j == ("s", 7):
+                        finish(4)
             if 0 <= step - 1 < n_tiles:
                 if tiles[step - 1][0] == "r":
                     turn(tiles[step - 1])

@@ -103,6 +103,7 @@ def tile_moe_shr_glu_relu_kernel(
         units = [(j, s) for j in tiles for s in range(PASSES)]
         batches = [units[0:4], units[4:8], units[8:12], units[12:16], units[16:20], units[20:22], units[22:23], units[23:24]]
         batch_of = {unit: (g, k) for g, members in enumerate(batches) for k, unit in enumerate(members)}
+        on_gpsimd = [(("s", k), 0) for k in (2, 4, 6)]
         hidden, turned, quantised, y_bank = {}, {}, {}, {}
 
         def hidden_rows(unit, count):
@@ -114,7 +115,12 @@ def tile_moe_shr_glu_relu_kernel(
         def gated_product(unit, h, a, b, read, write):
             relu_a = ring.tile([P, PASS], F32, name="relu_a", bufs=len(units))
             nc.scalar.activation(write(relu_a[:]), read(a), RELU)
-            nc.vector.tensor_tensor(write(h), read(b), write(relu_a[:]), MULT)
+            if unit in on_gpsimd:
+                b_copy = ring.tile([P, PASS], F32, name="b_copy", bufs=len(on_gpsimd))
+                nc.scalar.copy(write(b_copy[:]), read(b))
+                nc.gpsimd.tensor_tensor(h, b_copy[:], relu_a[:], MULT)
+            else:
+                nc.vector.tensor_tensor(write(h), read(b), write(relu_a[:]), MULT)
 
         def in_order(unit, for_a, for_b):
             return (for_a, for_b) if unit == units[0] else (for_b, for_a)

from contextlib import ExitStack

import concourse.mybir as mybir
from concourse.masks import make_identity

K, T, E, C, H, N = 512, 1024, 2, 256, 1024, 128
S = E * C

F32 = mybir.dt.float32
BF16 = mybir.dt.bfloat16
I32 = mybir.dt.int32
U32 = mybir.dt.uint32
U16 = mybir.dt.uint16
U8 = mybir.dt.uint8
FP8X4 = mybir.dt.float8_e4m3fn_x4
FP4X4 = mybir.dt.float4_e2m1fn_x4
MULT = mybir.AluOpType.mult
ADD = mybir.AluOpType.add
RELU = mybir.ActivationFunctionType.Relu

P = 128
PASS = 512
PASSES = H // PASS
FLOPS = 2 * (S + T) * (2 * K * H + H * N)


def tile_moe_shr_glu_relu_kernel(
    tc, x_words, x_scales, w1_words, w1_scales, w3_words, w3_scales, w2_words, w2_scales, gate, offs, out
):
    nc = tc.nc
    with ExitStack() as ctx:
        keep = ctx.enter_context(tc.tile_pool(name="keep", bufs=1))
        ring = ctx.enter_context(tc.tile_pool(name="ring", bufs=4))
        psum = ctx.enter_context(tc.psum_pool(name="psum", bufs=2))

        def zeroed_plane(engine, name, shape):
            plane = keep.tile(shape, U8, name=name, align_bytes=64)
            engine.memset(plane[:].bitcast(I32), 0)
            return plane

        def load_scale_rows(plane, rows, which):
            for r in which:
                nc.sync.dma_start(plane[r:P:32].bitcast(I32), rows[r:16:4].bitcast(I32))

        def load_words(words, src):
            nc.sync.dma_start(words.bitcast(I32), src.bitcast(I32))

        w1s = zeroed_plane(nc.gpsimd, "w1s", [P, E + 1, H])
        xs = zeroed_plane(nc.vector, "xs", [P, T])
        w3s = zeroed_plane(nc.vector, "w3s", [P, E + 1, H])
        w2s = zeroed_plane(nc.gpsimd, "w2s", [P, (E + 1) * PASSES, N])
        routed = keep.tile([P, T], F32, name="routed")
        nc.vector.memset(routed[:], 0.0)
        ident = keep.tile([P, P], F32, name="ident")
        make_identity(nc, ident[:])

        w1w_shared = keep.tile([P, 2 * H], U8, name="w1w_shared", align_bytes=64)
        w3w_shared = keep.tile([P, 2 * H], U8, name="w3w_shared", align_bytes=64)
        w1w_routed = keep.tile([P, E, 2 * H], U8, name="w1w_routed", align_bytes=64)
        w3w_routed = keep.tile([P, E, 2 * H], U8, name="w3w_routed", align_bytes=64)
        offsets = keep.tile([P, S // 16], U16, name="offsets")
        xw = keep.tile([P, T], I32, name="xw", align_bytes=64)
        load_words(w1w_shared[:], w1_words[E, 0])
        load_scale_rows(w1s, w1_scales[:, 0].rearrange("e q i -> q e i"), range(4))
        nc.sync.dma_start(offsets[:], offs)
        load_scale_rows(xs, x_scales[0], range(1))
        nc.sync.dma_start(xw[:], x_words[0].rearrange("p t r -> p (t r)").bitcast(I32))
        load_scale_rows(xs, x_scales[0], range(1, 4))
        load_words(w3w_shared[:], w3_words[E, 0])
        load_scale_rows(w3s, w3_scales[:, 0].rearrange("e q i -> q e i"), range(4))
        load_words(w1w_routed[:], w1_words[:E, 0].rearrange("e p c -> p e c"))
        load_words(w3w_routed[:], w3_words[:E, 0].rearrange("e p c -> p e c"))
        w2w = keep.tile([P, (E + 1) * PASSES, 2 * N], U8, name="w2w", align_bytes=64)
        load_words(w2w[:], w2_words.rearrange("e s p n -> p (e s) n"))
        load_scale_rows(w2s, w2_scales.rearrange("e s q n -> q (e s) n"), range(4))
        gates = keep.tile([P, S], F32, name="gates")
        nc.sync.dma_start(gates[:], gate)

        def regroup(name, columns, run):
            grouped = keep.tile(list(columns.shape), columns.dtype, name=name, align_bytes=64)
            nc.vector.tensor_copy(
                grouped[:].rearrange("p (g d b m) -> p g b d m", d=4, b=P // run, m=run),
                columns.rearrange("p (g b m d) -> p g b d m", d=4, b=P // run, m=run),
            )
            return grouped

        w1s_grouped = regroup("w1s_grouped", w1s[:, E], 16)
        w1w_grouped = regroup("w1w_grouped", w1w_shared[:].bitcast(U16), 8)
        w1_grouped, w3_grouped = [], []
        for s in range(PASSES):
            cols = slice(PASS * s, PASS * (s + 1))
            w1_grouped.append((w1w_grouped[:, cols], w1s_grouped[:, cols]))
            words = regroup(f"w3w_grouped{s}", w3w_shared[:].bitcast(U16)[:, cols], 8)
            scales = regroup(f"w3s_grouped{s}", w3s[:, E, cols], 16)
            w3_grouped.append((words[:], scales[:]))

        gw = keep.tile([P, S], I32, name="gw", align_bytes=64)
        gs = keep.tile([P, S], U8, name="gs", align_bytes=64)
        nc.vector.tensor_copy(gw[:].bitcast(U32), xw[:].bitcast(U32).indirect(offsets[:]))
        nc.vector.tensor_copy(gs[:], xs[:].indirect(offsets[:]))

        tiles = [("s", k) for k in range(2)] + [("r", k) for k in range(4)] + [("s", k) for k in range(2, 8)]
        units = [(j, s) for j in tiles for s in range(PASSES)]
        batches = [units[0:4], units[4:8], units[8:12], units[12:16], units[16:20], units[20:22], units[22:23], units[23:24]]
        batch_of = {unit: (g, k) for g, members in enumerate(batches) for k, unit in enumerate(members)}
        on_gpsimd = [(("s", k), 0) for k in (2, 4, 6)]
        hidden, turned, quantised, y_bank = {}, {}, {}, {}

        def hidden_rows(unit, count):
            g, k = batch_of[unit]
            if g not in turned:
                turned[g] = ring.tile([P, len(batches[g]) * PASS], BF16, name="ht", align_bytes=64, bufs=len(batches))
            return turned[g][:, PASS * k : PASS * (k + count)]

        def gated_product(unit, h, a, b, read, write):
            relu_a = ring.tile([P, PASS], F32, name="relu_a", bufs=len(units))
            nc.scalar.activation(write(relu_a[:]), read(a), RELU)
            if unit in on_gpsimd:
                b_copy = ring.tile([P, PASS], F32, name="b_copy", bufs=len(on_gpsimd))
                nc.scalar.copy(write(b_copy[:]), read(b))
                nc.gpsimd.tensor_tensor(h, b_copy[:], relu_a[:], MULT)
            else:
                nc.vector.tensor_tensor(write(h), read(b), write(relu_a[:]), MULT)

        def in_order(unit, for_a, for_b):
            return (for_a, for_b) if unit == units[0] else (for_b, for_a)

        def first_layer_routed(j):
            c = P * j[1]
            e = c // C
            words, scales = gw[:, c : c + P], gs[:, c : c + P]
            h = ring.tile([P, PASSES, PASS], BF16, name="h", align_bytes=64)
            for s in range(PASSES):
                a = psum.tile([P, PASS], F32, name="a", bufs=3)
                b = psum.tile([P, PASS], F32, name="b", bufs=3)
                for acc, ww, ws in in_order(
                    (j, s), (a, w1w_routed[:, e], w1s[:, e]), (b, w3w_routed[:, e], w3s[:, e])
                ):
                    nc.tensor.matmul_mx(
                        acc[:],
                        lhsT=words.bitcast(FP8X4),
                        lhsT_scale=scales,
                        rhs=ww[:, 2 * PASS * s : 2 * PASS * (s + 1)].bitcast(FP4X4),
                        rhs_scale=ws[:, PASS * s : PASS * (s + 1)],
                        start=True,
                        stop=True,
                    )
                gated_product(
                    (j, s),
                    h[:, s, :],
                    a[:],
                    b[:],
                    lambda ap: ap.rearrange("t (p u e) -> t u p e", u=2, e=2),
                    lambda ap: ap.rearrange("t (u p e) -> t u p e", u=2, e=2),
                )
            hidden[j] = h

        def first_layer_shared(j):
            words, scales = xw[:, P * j[1] : P * (j[1] + 1)], xs[:, P * j[1] : P * (j[1] + 1)]
            for s in range(PASSES):
                a = psum.tile([P, PASS], F32, name="a", bufs=3)
                b = psum.tile([P, PASS], F32, name="b", bufs=3)
                for acc, (ww, ws) in in_order((j, s), (a, w1_grouped[s]), (b, w3_grouped[s])):
                    for d in range(4):
                        cols = slice(P * d, P * (d + 1))
                        nc.tensor.matmul_mx(
                            acc[:, P * d : P * (d + 1)],
                            lhsT=ww[:, cols].bitcast(FP4X4),
                            lhsT_scale=ws[:, cols],
                            rhs=words.bitcast(FP8X4),
                            rhs_scale=scales,
                            start=True,
                            stop=True,
                        )
                gated_product(
                    (j, s),
                    hidden_rows((j, s), 1),
                    a[:],
                    b[:],
                    lambda ap: ap.rearrange("p (d t) -> p t d", d=4),
                    lambda ap: ap.rearrange("p (t d) -> p t d", d=4),
                )

        def turn(j):
            h = hidden[j]
            t_ps = psum.tile([P, PASS], F32, name="t_ps", tag="turn", bufs=1)
            for s in range(PASSES):
                pairs = h[:, s, :].bitcast(F32)
                for u in range(2):
                    nc.tensor.transpose(
                        t_ps[:, P * (2 * s + u) : P * (2 * s + u + 1)], pairs[:, P * u : P * (u + 1)], ident[:]
                    )
            nc.scalar.copy(
                hidden_rows((j, 0), PASSES).bitcast(F32).rearrange("p (s t u) -> p s t u", s=PASSES, u=2),
                t_ps[:].rearrange("p (s u t) -> p s t u", s=PASSES, u=2),
            )

        def quantise(g):
            width = len(batches[g]) * P
            codes = ring.tile([P, width], U32, name="codes", align_bytes=64, bufs=len(batches))
            scales = ring.tile([P, width], U8, name="h_scales", align_bytes=64, bufs=len(batches))
            nc.vector.quantize_mx(codes[:].bitcast(FP8X4), scales[:], turned[g][:])
            for k, unit in enumerate(batches[g]):
                quantised[unit] = (codes[:, P * k : P * (k + 1)], scales[:, P * k : P * (k + 1)])

        groups = [
            ([("s", k) for k in range(0, 2)], "y"),
            ([("r", k) for k in range(0, 4)], "y"),
            ([("s", k) for k in range(2, 6)], "y"),
            ([("s", 6)], "turn"),
            ([("s", 7)], "y"),
        ]
        place = {j: (g, k) for g, (members, tag) in enumerate(groups) for k, j in enumerate(members)}

        def second_layer(j):
            g, k = place[j]
            if k == 0:
                y_bank[g] = psum.tile([P, PASS], F32, name="y", tag=groups[g][1], bufs=1)
            e = E if j[0] == "s" else P * j[1] // C
            for s in range(PASSES):
                codes, scales = quantised[(j, s)]
                nc.tensor.matmul_mx(
                    y_bank[g][:, P * k : P * (k + 1)],
                    lhsT=w2w[:, PASSES * e + s, :].bitcast(FP4X4),
                    lhsT_scale=w2s[:, PASSES * e + s, :],
                    rhs=codes.bitcast(FP8X4),
                    rhs_scale=scales,
                    start=(s == 0),
                    stop=(s == PASSES - 1),
                )

        def scatter(e):
            cols = slice(C * e, C * (e + 1))
            y_slots = keep.tile([P, C], F32, name=f"y_slots{e}")
            nc.scalar.copy(y_slots[:], y_bank[1][:, cols])
            piece = offsets[:, C * e // 16 : C * (e + 1) // 16]
            nc.vector.tensor_tensor(routed[:].indirect(piece), y_slots[:], gates[:, cols], MULT)

        def finish(g):
            members = groups[g][0]
            width = P * len(members)
            c0 = P * members[0][1]
            result = keep.tile([P, width], F32, name=f"result{g}")
            shared_part = early[:] if g == 0 else y_bank[g][:, :width]
            nc.vector.tensor_tensor(result[:], shared_part, routed[:, c0 : c0 + width], ADD)
            nc.sync.dma_start(out[:, c0 : c0 + width], result[:])

        early = keep.tile([P, 2 * P], F32, name="early")
        n_tiles = len(tiles)
        done = []
        for step in range(n_tiles + 2):
            if step < n_tiles:
                if tiles[step][0] == "r":
                    first_layer_routed(tiles[step])
                else:
                    first_layer_shared(tiles[step])
            for j in tiles:
                if j not in done and (j, PASSES - 1) in quantised:
                    done.append(j)
                    second_layer(j)
                    if j == ("s", 1):
                        nc.scalar.copy(early[:], y_bank[0][:, : 2 * P])
                    if j == ("r", 1):
                        scatter(0)
                    if j == ("r", 3):
                        scatter(1)
                        finish(0)
                    if j == ("s", 5):
                        finish(2)
                    if j == ("s", 6):
                        finish(3)
                    if j == ("s", 7):
                        finish(4)
            if 0 <= step - 1 < n_tiles:
                if tiles[step - 1][0] == "r":
                    turn(tiles[step - 1])
                for g, members in enumerate(batches):
                    if members[-1][0] == tiles[step - 1]:
                        quantise(g)
